import numpy as np
import ml_dtypes


def mxq(x, axis, fmt="e4m3"):
    dtype, down = {"e4m3": (ml_dtypes.float8_e4m3fn, 7), "e5m2": (ml_dtypes.float8_e5m2, 14)}[fmt]
    v = np.moveaxis(np.asarray(x, np.float32).astype(ml_dtypes.bfloat16).astype(np.float64), axis, -1)
    blocks = v.reshape(v.shape[:-1] + (-1, 32))
    amax = np.abs(blocks).max(-1, keepdims=True)
    byte = np.maximum(np.where(amax > 0, np.frexp(amax)[1] - 1 + 127, 0) - down, 1)
    scale = np.exp2(byte - 127.0)
    codes = (blocks / scale).astype(np.float32).astype(dtype).astype(np.float64)
    return np.moveaxis((codes * scale).reshape(v.shape), -1, axis)


WIDE = False


def mx_kscale(k):
    if not WIDE:
        return np.ones(k)
    levels = np.array([10, -10, 5, -5, 0])
    if k % 512:
        return np.exp2(np.random.permutation(np.resize(levels, k // 32))).repeat(32)
    a = np.empty((k // 512, 16))
    for p in range(k // 512):
        a[p, :8] = np.random.permutation(np.resize(levels, 8))
        for g in range(8):
            far = levels[np.abs(levels - a[p, g]) >= 10]
            a[p, g + 8] = far[np.random.randint(len(far))]
    return np.exp2(a.ravel()).repeat(32)


def f64(x):
    return np.asarray(x).astype(np.float64)


def striped(idx):
    return np.tile(np.asarray(idx).reshape(-1, 16).T, (8, 1)).astype(np.uint16)


def unstriped(offs):
    return offs[:16].T.reshape(-1).astype(np.int64)


E2M1 = np.array([0.0, 0.5, 1.0, 1.5, 2.0, 3.0, 4.0, 6.0, -0.0, -0.5, -1.0, -1.5, -2.0, -3.0, -4.0, -6.0])


def pack_weight(w, fmt):
    k, n = w.shape
    w = f64(np.asarray(w, np.float32).astype(ml_dtypes.bfloat16)).reshape(k // 32, 32, n)
    amax = np.abs(w).max(1)
    if fmt == "e4m3":
        byte = np.frexp(amax)[1] - 1 + 127 - 7
    else:
        mant, ex = np.frexp(amax / 6.0)
        byte = np.where(mant > 0.5, ex, ex - 1) + 127
    byte = np.clip(np.where(amax > 0, byte, 1), 1, 254)
    scaled = (w * np.exp2(127.0 - byte)[:, None, :]).reshape(k, n).astype(np.float32)
    by_word = np.ascontiguousarray(scaled.reshape(k // 512, 128, 4, n).transpose(0, 1, 3, 2))
    if fmt == "e4m3":
        words = by_word.astype(ml_dtypes.float8_e4m3fn).view(np.uint8)
    else:
        c = by_word.astype(ml_dtypes.float4_e2m1fn).view(np.uint8) & 0xF
        words = (c[..., 0::2] | (c[..., 1::2] << 4)).reshape(k // 512, 128, 2 * n)
    return np.ascontiguousarray(words), np.ascontiguousarray(byte.astype(np.uint8).reshape(k // 512, 16, n))


def unpack_weight(words, scales, fmt):
    g, _, n = scales.shape
    words = np.ascontiguousarray(words).reshape(g, 128, n, -1)
    if fmt == "e4m3":
        vals = words.view(ml_dtypes.float8_e4m3fn).astype(np.float64)
    else:
        nib = np.empty((g, 128, n, 4), np.uint8)
        nib[..., 0::2] = words & 0xF
        nib[..., 1::2] = words >> 4
        vals = E2M1[nib]
    vals = vals * np.repeat(np.exp2(scales.astype(np.float64) - 127.0), 8, axis=1)[..., None]
    return vals.transpose(0, 1, 3, 2).reshape(g * 512, n)


def sigmoid(v):
    return 1.0 / (1.0 + np.exp(-v))


def sgn(shape):
    return np.random.uniform(0.5, 2.0, shape) * np.where(np.random.standard_normal(shape) < 0, -1.0, 1.0)


K, T, J, R, F, Z, C, O, N, L, E = 512, 1024, 256, 512, 512, 1024, 512, 128, 256, 512, 1024


def setup_inputs():
    n = np.random.standard_normal
    idx = np.random.permutation(T)[:J]
    idx2 = np.random.permutation(Z)[:J]
    idx3 = np.random.permutation(C)[:J]
    idx4 = np.random.permutation(C)[:J]
    idx5 = np.random.permutation(J)[:O]
    idx6 = np.random.permutation(J)[:O]
    idx7 = np.random.permutation(E)[:O]
    ff = mx_kscale(F)
    fk = mx_kscale(K)
    fr = mx_kscale(R)
    fl = mx_kscale(L)
    xop = pack_weight(n((F, Z)) / ff[:, None], "e4m3")
    wp = pack_weight(n((K, R)) * 1 / np.sqrt(K) / fk[:, None], "e2m1")
    w2p = pack_weight(n((F, R)) * 1 / np.sqrt(F) * ff[:, None], "e2m1")
    wbp = pack_weight(n((R, N)) * 1 / np.sqrt(R) / fr[:, None], "e2m1")
    sxp = pack_weight(n((L, O)) / fl[:, None], "e4m3")
    wsp = pack_weight(n((L, N)) * 1 / np.sqrt(L) * fl[:, None], "e2m1")
    return {
        "xo_words": xop[0],
        "xo_scales": xop[1],
        "cq": (np.random.randint(-7, 8, (K, T)).astype(np.float64)).astype(np.float32),
        "gs": (np.random.uniform(0.1, 0.4, (K, 1)) * fk[:, None]).astype(np.float32),
        "w_words": wp[0],
        "w_scales": wp[1],
        "w2_words": w2p[0],
        "w2_scales": w2p[1],
        "sa": (np.random.uniform(0.5, 1.6, (R, 1))).astype(np.float32),
        "sb": (np.random.uniform(0.5, 1.6, (R, 1)) * fr[:, None]).astype(np.float32),
        "sg": (sgn((R, 1))).astype(np.float32),
        "bg": (np.random.uniform(-2.0, 2.0, (R, 1))).astype(np.float32),
        "wb_words": wbp[0],
        "wb_scales": wbp[1],
        "sx_words": sxp[0],
        "sx_scales": sxp[1],
        "ws_words": wsp[0],
        "ws_scales": wsp[1],
        "offs": striped(idx),
        "offs2": striped(idx2),
        "offs3": striped(idx3),
        "offs4": striped(idx4),
        "offs5": striped(idx5),
        "offs6": striped(idx6),
        "offs7": striped(idx7),
    }


def reference(xo_words, xo_scales, cq, gs, w_words, w_scales, w2_words, w2_scales, sa, sb, sg, bg, wb_words, wb_scales, sx_words, sx_scales, ws_words, ws_scales, offs, offs2, offs3, offs4, offs5, offs6, offs7):
    idx = unstriped(offs)
    idx2 = unstriped(offs2)
    idx3 = unstriped(offs3)
    idx4 = unstriped(offs4)
    idx5 = unstriped(offs5)
    idx6 = unstriped(offs6)
    idx7 = unstriped(offs7)
    xou = unpack_weight(xo_words, xo_scales, "e4m3")
    wu = unpack_weight(w_words, w_scales, "e2m1")
    w2u = unpack_weight(w2_words, w2_scales, "e2m1")
    wbu = unpack_weight(wb_words, wb_scales, "e2m1")
    sxu = unpack_weight(sx_words, sx_scales, "e4m3")
    wsu = unpack_weight(ws_words, ws_scales, "e2m1")
    x1 = f64(cq)[:, idx] * f64(gs)
    x1q = mxq(x1, 0, "e4m3")
    a = wu.T @ x1q
    xoidx2g = xou[:, idx2]
    b = w2u.T @ xoidx2g
    pw = np.zeros((R, C))
    pw[:, idx3] = a
    rb = np.maximum(pw[:, idx4] * f64(sa), b)
    hid = rb[:, idx5] * f64(sb) * sigmoid(rb[:, idx6] * f64(sg) + f64(bg))
    hidq = mxq(hid, 0, "e4m3")
    p = wbu.T @ hidq + wsu.T @ sxu
    y = np.zeros((N, E))
    y[:, idx7] = p
    return y

@@ -1,0 +1,267 @@
+from contextlib import ExitStack
+
+import concourse.mybir as mybir
+
+K, T, J, R, F, Z, C, O, N, L, E = 512, 1024, 256, 512, 512, 1024, 512, 128, 256, 512, 1024
+
+FLOPS = 2 * (K * R * J + F * R * J + R * N * O + L * N * O)
+
+F32 = mybir.dt.float32
+BF16 = mybir.dt.bfloat16
+I32 = mybir.dt.int32
+U32 = mybir.dt.uint32
+U16 = mybir.dt.uint16
+U8 = mybir.dt.uint8
+FP8X4 = mybir.dt.float8_e4m3fn_x4
+FP4X4 = mybir.dt.float4_e2m1fn_x4
+ACT = mybir.ActivationFunctionType
+ALU = mybir.AluOpType
+
+P = 128
+PACK = 4
+QUADS = 4
+QROWS = 32
+LIVE = 4
+
+
+def tile_list_gatedanswer_codednote_further_scattered_kernel(
+    tc, xo_words, xo_scales, cq, gs, w_words, w_scales, w2_words, w2_scales, sa, sb, sg, bg,
+    wb_words, wb_scales, sx_words, sx_scales, ws_words, ws_scales,
+    offs, offs2, offs3, offs4, offs5, offs6, offs7, out,
+):
+    nc = tc.nc
+    with ExitStack() as ctx:
+        pool = ctx.enter_context(tc.tile_pool(name="held", bufs=1))
+        psum = ctx.enter_context(tc.psum_pool(name="psum", bufs=1))
+
+        def new(shape, dtype, name, tag=None):
+            return pool.tile(shape, dtype, name=name, tag=tag or name, align_bytes=64)
+
+        def load_list(src, name):
+            lst = new(list(src.shape), U16, name)
+            nc.sync.dma_start(lst[:], src)
+            return lst
+
+        def load_rows(src, name):
+            vec = new([P, PACK], F32, name)
+            nc.sync.dma_start(vec[:], src.rearrange("(p t) o -> p (t o)", t=PACK))
+            return vec
+
+        def load_fp4(src, name):
+            words = new([P, src.shape[2]], U8, name)
+            nc.sync.dma_start(words[:].bitcast(I32), src[0].bitcast(I32))
+            return words
+
+        def load_fp8(src, name):
+            words = new([P, src.shape[2]], U32, name)
+            nc.sync.dma_start(words[:].bitcast(I32), src[0].rearrange("p n t -> p (n t)").bitcast(I32))
+            return words
+
+        def load_cq(t):
+            rows = new([P, T], F32, "cq%d" % t)
+            nc.sync.dma_start(rows[:], cq.rearrange("(p t) c -> t p c", t=PACK)[t])
+            return rows
+
+        def stage_scales(src, stage, first):
+            nc.sync.dma_start(
+                stage[first:first + LIVE, :, :],
+                src[0].bitcast(I32).rearrange("(q r) n -> r q n", r=LIVE),
+            )
+
+        def load_plane(src, name):
+            plane = new([P, src.shape[2]], U8, name)
+            nc.vector.memset(plane[:].bitcast(I32), 0)
+            for q in range(QUADS):
+                nc.sync.dma_start(
+                    plane[QROWS * q:QROWS * q + LIVE, :].bitcast(I32),
+                    src[0, LIVE * q:LIVE * (q + 1), :].bitcast(I32),
+                )
+            return plane
+
+        xo_stage = new([LIVE, QUADS, Z // 4], I32, "xo_stage")
+        w_stage = new([LIVE, QUADS, R // 4], I32, "w_stage")
+        w2_stage = new([LIVE, QUADS, R // 4], I32, "w2_stage")
+
+        cq_t = [load_cq(0)]
+        l1 = load_list(offs, "l1")
+        gs_t = load_rows(gs, "gs_t")
+        cq_t.append(load_cq(1))
+        stage_scales(w_scales, w_stage, 0)
+        w_raw = load_fp4(w_words, "w_raw")
+        stage_scales(xo_scales, xo_stage, 0)
+        cq_t.append(load_cq(2))
+        l2 = load_list(offs2, "l2")
+        stage_scales(w2_scales, w2_stage, 0)
+        cq_t.append(load_cq(3))
+        w2_raw = load_fp4(w2_words, "w2_raw")
+        xo_w = load_fp8(xo_words, "xo_w")
+        l3 = load_list(offs3, "l3")
+        l4 = load_list(offs4, "l4")
+        sa_t = load_rows(sa, "sa_t")
+        l5 = load_list(offs5, "l5")
+        sb_t = load_rows(sb, "sb_t")
+        l6 = load_list(offs6, "l6")
+        sg_t = load_rows(sg, "sg_t")
+        bg_t = load_rows(bg, "bg_t")
+        ws_w = load_fp4(ws_words, "ws_w")
+        sx_w = load_fp8(sx_words, "sx_w")
+        wb_w = load_fp4(wb_words, "wb_w")
+        l7 = load_list(offs7, "l7")
+        ws_s = load_plane(ws_scales, "ws_s")
+        sx_s = load_plane(sx_scales, "sx_s")
+        wb_s = load_plane(wb_scales, "wb_s")
+
+        def deal_scales(stage, name):
+            raw = new([P, R], U8, name + "_raw")
+            nc.vector.memset(raw[:].bitcast(I32), 0)
+            for q in range(QUADS):
+                nc.vector.tensor_copy(raw[QROWS * q:QROWS * q + LIVE, :].bitcast(I32), stage[:, q, :])
+            dealt = new([P, R], U8, name)
+            nc.vector.tensor_copy(
+                dealt[:].rearrange("p (t c i) -> p c t i", t=PACK, i=16),
+                raw[:].rearrange("p (c i t) -> p c t i", t=PACK, i=16),
+            )
+            return dealt
+
+        def deal_words(raw, name):
+            dealt = new([P, 2 * R], U8, name)
+            nc.scalar.copy(
+                dealt[:].bitcast(U16).rearrange("p (t c i) -> p c t i", t=PACK, i=8),
+                raw[:].bitcast(U16).rearrange("p (c i t) -> p c t i", t=PACK, i=8),
+            )
+            return dealt
+
+        w_s = deal_scales(w_stage, "w_s")
+
+        xo_s = new([P, Z], U8, "xo_s")
+        nc.vector.memset(xo_s[:].bitcast(I32), 0)
+        for q in range(QUADS):
+            nc.vector.tensor_copy(xo_s[QROWS * q:QROWS * q + LIVE, :].bitcast(I32), xo_stage[:, q, :])
+        xg_s = new([P, J], U8, "xg_s")
+        nc.vector.tensor_copy(xg_s[:], xo_s[:].indirect(l2[:]))
+
+        w2_s = deal_scales(w2_stage, "w2_s")
+
+        x1 = new([P, PACK, J], BF16, "x1")
+        x1_il = new([P, J, PACK], BF16, "x1_il")
+        x1_c = new([P, J], U32, "x1_c")
+        x1_s = new([P, J], U8, "x1_s")
+        w_d = None
+        for t in range(PACK):
+            nc.scalar.activation(
+                out=x1[:, t, :], in_=cq_t[t][:].indirect(l1[:]), func=ACT.Copy, scale=gs_t[:, t:t + 1],
+            )
+            if t == 1:
+                w_d = deal_words(w_raw, "w_d")
+        halves = [slice(0, J // 2), slice(J // 2, J)]
+        for h in halves:
+            nc.vector.tensor_copy(
+                x1_il[:, h, :].rearrange("p (c i) t -> p c t i", i=4),
+                x1[:, :, h].rearrange("p t (c i) -> p c t i", i=4),
+            )
+        for h in halves:
+            nc.vector.quantize_mx(
+                out=x1_c[:, h].bitcast(FP8X4), scales=x1_s[:, h],
+                in_=x1_il[:, h, :].rearrange("p j t -> p (j t)"),
+            )
+        w2_d = deal_words(w2_raw, "w2_d")
+
+        a_ps = [psum.tile([P, J], F32, name="a_ps%d" % t, tag="a_ps%d" % t) for t in range(PACK)]
+        for t in range(PACK):
+            nc.tensor.matmul_mx(
+                out=a_ps[t][:], lhsT=w_d[:, 2 * P * t:2 * P * (t + 1)].bitcast(FP4X4),
+                lhsT_scale=w_s[:, P * t:P * (t + 1)], rhs=x1_c[:].bitcast(FP8X4), rhs_scale=x1_s[:],
+                start=True, stop=True,
+            )
+
+        xg_w = new([P, J], U32, "xg_w")
+        nc.vector.tensor_copy(xg_w[:], xo_w[:].indirect(l2[:]))
+        b_ps = [psum.tile([P, J], F32, name="b_ps%d" % t) for t in range(PACK)]
+        for t in range(PACK):
+            nc.tensor.matmul_mx(
+                out=b_ps[t][:], lhsT=w2_d[:, 2 * P * t:2 * P * (t + 1)].bitcast(FP4X4),
+                lhsT_scale=w2_s[:, P * t:P * (t + 1)], rhs=xg_w[:].bitcast(FP8X4), rhs_scale=xg_s[:],
+                start=True, stop=True,
+            )
+
+        pw = [new([P, C], F32, "pw%d" % t) for t in range(PACK)]
+        picked = [new([P, J], F32, "picked%d" % t) for t in range(PACK)]
+        rb = [new([P, J], F32, "rb%d" % t) for t in range(PACK)]
+        val = new([P, PACK, O], F32, "val")
+        gate = new([P, PACK, O], F32, "gate")
+        for t in range(PACK):
+            nc.vector.memset(pw[t][:], 0.0)
+
+        def pick(t):
+            nc.scalar.activation(out=picked[t][:], in_=pw[t][:].indirect(l4[:]), func=ACT.Copy, scale=sa_t[:, t:t + 1])
+
+        def larger(t):
+            nc.vector.tensor_tensor(out=rb[t][:], in0=b_ps[t][:], in1=picked[t][:], op=ALU.max)
+
+        def look(t):
+            nc.scalar.activation(out=val[:, t, :], in_=rb[t][:].indirect(l5[:]), func=ACT.Copy, scale=sb_t[:, t:t + 1])
+            nc.scalar.activation(
+                out=gate[:, t, :], in_=rb[t][:].indirect(l6[:]), func=ACT.Sigmoid,
+                scale=sg_t[:, t:t + 1], bias=bg_t[:, t:t + 1],
+            )
+
+        half = J // 2
+        a_sb = [new([P, J], F32, "a_sb%d" % t, "xo_w" if t == 0 else None) for t in range(PACK)]
+        nc.vector.tensor_copy(a_sb[0][:], a_ps[0][:])
+        nc.scalar.copy(a_sb[1][:], a_ps[1][:])
+        nc.vector.tensor_copy(pw[0][:].indirect(l3[:]), a_sb[0][:])
+        nc.scalar.activation(out=pw[1][:].indirect(l3[:]), in_=a_sb[1][:], func=ACT.Copy)
+        nc.vector.tensor_copy(a_sb[2][:], a_ps[2][:])
+        nc.vector.tensor_copy(a_sb[3][:], a_ps[3][:])
+        nc.vector.tensor_copy(pw[2][:].indirect(l3[:]), a_sb[2][:])
+        pick(0)
+        pick(1)
+        nc.scalar.activation(out=pw[3][:].indirect(l3[:, 0:half // 16]), in_=a_sb[3][:, 0:half], func=ACT.Copy)
+        larger(0)
+        nc.vector.tensor_copy(pw[3][:].indirect(l3[:, half // 16:J // 16]), a_sb[3][:, half:J])
+        pick(2)
+        look(0)
+        larger(1)
+        pick(3)
+        larger(2)
+        larger(3)
+        for t in range(1, PACK):
+            look(t)
+
+        hid_il = new([P, O, PACK], BF16, "hid_il")
+        nc.vector.tensor_tensor(
+            out=hid_il[:].rearrange("p (c i) t -> p c t i", i=4),
+            in0=val[:].rearrange("p t (c i) -> p c t i", i=4),
+            in1=gate[:].rearrange("p t (c i) -> p c t i", i=4),
+            op=ALU.mult,
+        )
+        hid_c = new([P, O], U32, "hid_c")
+        hid_s = new([P, O], U8, "hid_s")
+        nc.vector.quantize_mx(
+            out=hid_c[:].bitcast(FP8X4), scales=hid_s[:], in_=hid_il[:].rearrange("p o t -> p (o t)"),
+        )
+
+        p_ps = [psum.tile([P, O], F32, name="p_ps%d" % h, tag="a_ps%d" % (2 + h)) for h in range(N // P)]
+        for h in range(N // P):
+            nc.tensor.matmul_mx(
+                out=p_ps[h][:], lhsT=ws_w[:, 2 * P * h:2 * P * (h + 1)].bitcast(FP4X4),
+                lhsT_scale=ws_s[:, P * h:P * (h + 1)], rhs=sx_w[:].bitcast(FP8X4), rhs_scale=sx_s[:],
+                start=True, stop=False,
+            )
+        for h in range(N // P):
+            nc.tensor.matmul_mx(
+                out=p_ps[h][:], lhsT=wb_w[:, 2 * P * h:2 * P * (h + 1)].bitcast(FP4X4),
+                lhsT_scale=wb_s[:, P * h:P * (h + 1)], rhs=hid_c[:].bitcast(FP8X4), rhs_scale=hid_s[:],
+                start=False, stop=True,
+            )
+
+        page = [new([P, E], F32, "page%d" % h) for h in range(N // P)]
+        p_sb = [new([P, O], F32, "p_sb%d" % h) for h in range(N // P)]
+        for h in range(N // P):
+            nc.vector.memset(page[h][:], 0.0)
+        nc.vector.tensor_copy(p_sb[0][:], p_ps[0][:])
+        nc.vector.tensor_copy(page[0][:].indirect(l7[:]), p_sb[0][:])
+        nc.scalar.copy(p_sb[1][:], p_ps[1][:])
+        nc.scalar.activation(out=page[1][:].indirect(l7[:]), in_=p_sb[1][:], func=ACT.Copy)
+        for h in range(N // P):
+            nc.sync.dma_start(out[P * h:P * (h + 1), :], page[h][:])

@@ -111,6 +111,10 @@ def tile_list_gatedanswer_codednote_further_scattered_kernel(
         sx_s = load_plane(sx_scales, "sx_s")
         wb_s = load_plane(wb_scales, "wb_s")
 
+        warm = new([P, 2], F32, "warm")
+        nc.vector.memset(warm[:, 0:1], 0.0)
+        nc.scalar.activation(out=warm[:, 1:2], in_=warm[:, 0:1], func=ACT.Sigmoid)
+
         def deal_scales(stage, name):
             raw = new([P, R], U8, name + "_raw")
             nc.vector.memset(raw[:].bitcast(I32), 0)

@@ -62,39 +62,35 @@ def tile_list_gatedanswer_codednote_further_scattered_kernel(
             nc.sync.dma_start(rows[:], cq.rearrange("(p t) c -> t p c", t=PACK)[t])
             return rows
 
-        def stage_scales(src, stage, first):
-            nc.sync.dma_start(
-                stage[first:first + LIVE, :, :],
-                src[0].bitcast(I32).rearrange("(q r) n -> r q n", r=LIVE),
-            )
-
-        def load_plane(src, name):
+        def new_plane(src, name):
             plane = new([P, src.shape[2]], U8, name)
             nc.vector.memset(plane[:].bitcast(I32), 0)
-            for q in range(QUADS):
-                nc.sync.dma_start(
-                    plane[QROWS * q:QROWS * q + LIVE, :].bitcast(I32),
-                    src[0, LIVE * q:LIVE * (q + 1), :].bitcast(I32),
-                )
             return plane
 
-        xo_stage = new([LIVE, QUADS, Z // 4], I32, "xo_stage")
-        w_stage = new([LIVE, QUADS, R // 4], I32, "w_stage")
-        w2_stage = new([LIVE, QUADS, R // 4], I32, "w2_stage")
+        def load_plane(plane, src):
+            rows = src[0].bitcast(I32).rearrange("(q r) n -> r q n", r=LIVE)
+            for r in range(LIVE):
+                nc.sync.dma_start(plane[r:P:QROWS, :].bitcast(I32), rows[r])
+
+        xo_s = new_plane(xo_scales, "xo_s")
+        ws_s = new_plane(ws_scales, "ws_s")
+        sx_s = new_plane(sx_scales, "sx_s")
+        wb_s = new_plane(wb_scales, "wb_s")
+        stage = new([LIVE, QUADS, 2, R // 4], I32, "stage")
 
         cq_t = [load_cq(0)]
         l1 = load_list(offs, "l1")
         gs_t = load_rows(gs, "gs_t")
+        for s, src in enumerate((w_scales, w2_scales)):
+            nc.sync.dma_start(stage[:, :, s, :], src[0].bitcast(I32).rearrange("(q r) n -> r q n", r=LIVE))
         cq_t.append(load_cq(1))
-        stage_scales(w_scales, w_stage, 0)
-        w_raw = load_fp4(w_words, "w_raw")
-        stage_scales(xo_scales, xo_stage, 0)
         cq_t.append(load_cq(2))
         l2 = load_list(offs2, "l2")
-        stage_scales(w2_scales, w2_stage, 0)
         cq_t.append(load_cq(3))
-        w2_raw = load_fp4(w2_words, "w2_raw")
+        load_plane(xo_s, xo_scales)
+        w_raw = load_fp4(w_words, "w_raw")
         xo_w = load_fp8(xo_words, "xo_w")
+        w2_raw = load_fp4(w2_words, "w2_raw")
         l3 = load_list(offs3, "l3")
         l4 = load_list(offs4, "l4")
         sa_t = load_rows(sa, "sa_t")
@@ -107,23 +103,27 @@ def tile_list_gatedanswer_codednote_further_scattered_kernel(
         sx_w = load_fp8(sx_words, "sx_w")
         wb_w = load_fp4(wb_words, "wb_w")
         l7 = load_list(offs7, "l7")
-        ws_s = load_plane(ws_scales, "ws_s")
-        sx_s = load_plane(sx_scales, "sx_s")
-        wb_s = load_plane(wb_scales, "wb_s")
+        load_plane(ws_s, ws_scales)
+        load_plane(sx_s, sx_scales)
+        load_plane(wb_s, wb_scales)
 
         warm = new([P, 2], F32, "warm")
         nc.vector.memset(warm[:, 0:1], 0.0)
         nc.scalar.activation(out=warm[:, 1:2], in_=warm[:, 0:1], func=ACT.Sigmoid)
 
-        def deal_scales(stage, name):
-            raw = new([P, R], U8, name + "_raw")
-            nc.vector.memset(raw[:].bitcast(I32), 0)
-            for q in range(QUADS):
-                nc.vector.tensor_copy(raw[QROWS * q:QROWS * q + LIVE, :].bitcast(I32), stage[:, q, :])
+        raw_s = new([P, 2, R], U8, "raw_s")
+        raw_words = raw_s[:].rearrange("p s c -> p (s c)").bitcast(I32)
+        nc.vector.memset(raw_words, 0)
+        for q in range(QUADS):
+            nc.vector.tensor_copy(
+                raw_words[QROWS * q:QROWS * q + LIVE, :], stage[:, q, :, :].rearrange("p s c -> p (s c)"),
+            )
+
+        def deal_scales(s, name):
             dealt = new([P, R], U8, name)
             nc.vector.tensor_copy(
                 dealt[:].rearrange("p (t c i) -> p c t i", t=PACK, i=16),
-                raw[:].rearrange("p (c i t) -> p c t i", t=PACK, i=16),
+                raw_s[:, s, :].rearrange("p (c i t) -> p c t i", t=PACK, i=16),
             )
             return dealt
 
@@ -135,28 +135,20 @@ def tile_list_gatedanswer_codednote_further_scattered_kernel(
             )
             return dealt
 
-        w_s = deal_scales(w_stage, "w_s")
-
-        xo_s = new([P, Z], U8, "xo_s")
-        nc.vector.memset(xo_s[:].bitcast(I32), 0)
-        for q in range(QUADS):
-            nc.vector.tensor_copy(xo_s[QROWS * q:QROWS * q + LIVE, :].bitcast(I32), xo_stage[:, q, :])
+        w_s = deal_scales(0, "w_s")
+        w2_s = deal_scales(1, "w2_s")
         xg_s = new([P, J], U8, "xg_s")
         nc.vector.tensor_copy(xg_s[:], xo_s[:].indirect(l2[:]))
-
-        w2_s = deal_scales(w2_stage, "w2_s")
 
         x1 = new([P, PACK, J], BF16, "x1")
         x1_il = new([P, J, PACK], BF16, "x1_il")
         x1_c = new([P, J], U32, "x1_c")
         x1_s = new([P, J], U8, "x1_s")
-        w_d = None
         for t in range(PACK):
             nc.scalar.activation(
                 out=x1[:, t, :], in_=cq_t[t][:].indirect(l1[:]), func=ACT.Copy, scale=gs_t[:, t:t + 1],
             )
-            if t == 1:
-                w_d = deal_words(w_raw, "w_d")
+        w_d = deal_words(w_raw, "w_d")
         halves = [slice(0, J // 2), slice(J // 2, J)]
         for h in halves:
             nc.vector.tensor_copy(

from contextlib import ExitStack

import concourse.mybir as mybir

K, T, J, R, F, Z, C, O, N, L, E = 512, 1024, 256, 512, 512, 1024, 512, 128, 256, 512, 1024

FLOPS = 2 * (K * R * J + F * R * J + R * N * O + L * N * O)

F32 = mybir.dt.float32
BF16 = mybir.dt.bfloat16
I32 = mybir.dt.int32
U32 = mybir.dt.uint32
U16 = mybir.dt.uint16
U8 = mybir.dt.uint8
FP8X4 = mybir.dt.float8_e4m3fn_x4
FP4X4 = mybir.dt.float4_e2m1fn_x4
ACT = mybir.ActivationFunctionType
ALU = mybir.AluOpType

P = 128
PACK = 4
QUADS = 4
QROWS = 32
LIVE = 4


def tile_list_gatedanswer_codednote_further_scattered_kernel(
    tc, xo_words, xo_scales, cq, gs, w_words, w_scales, w2_words, w2_scales, sa, sb, sg, bg,
    wb_words, wb_scales, sx_words, sx_scales, ws_words, ws_scales,
    offs, offs2, offs3, offs4, offs5, offs6, offs7, out,
):
    nc = tc.nc
    with ExitStack() as ctx:
        pool = ctx.enter_context(tc.tile_pool(name="held", bufs=1))
        psum = ctx.enter_context(tc.psum_pool(name="psum", bufs=1))

        def new(shape, dtype, name, tag=None):
            return pool.tile(shape, dtype, name=name, tag=tag or name, align_bytes=64)

        def load_list(src, name):
            lst = new(list(src.shape), U16, name)
            nc.sync.dma_start(lst[:], src)
            return lst

        def load_rows(src, name):
            vec = new([P, PACK], F32, name)
            nc.sync.dma_start(vec[:], src.rearrange("(p t) o -> p (t o)", t=PACK))
            return vec

        def load_fp4(src, name):
            words = new([P, src.shape[2]], U8, name)
            nc.sync.dma_start(words[:].bitcast(I32), src[0].bitcast(I32))
            return words

        def load_fp8(src, name):
            words = new([P, src.shape[2]], U32, name)
            nc.sync.dma_start(words[:].bitcast(I32), src[0].rearrange("p n t -> p (n t)").bitcast(I32))
            return words

        def load_cq(t):
            rows = new([P, T], F32, "cq%d" % t)
            nc.sync.dma_start(rows[:], cq.rearrange("(p t) c -> t p c", t=PACK)[t])
            return rows

        def new_plane(src, name):
            plane = new([P, src.shape[2]], U8, name)
            nc.vector.memset(plane[:].bitcast(I32), 0)
            return plane

        def load_plane(plane, src):
            rows = src[0].bitcast(I32).rearrange("(q r) n -> r q n", r=LIVE)
            for r in range(LIVE):
                nc.sync.dma_start(plane[r:P:QROWS, :].bitcast(I32), rows[r])

        xo_s = new_plane(xo_scales, "xo_s")
        ws_s = new_plane(ws_scales, "ws_s")
        sx_s = new_plane(sx_scales, "sx_s")
        wb_s = new_plane(wb_scales, "wb_s")
        stage = new([LIVE, QUADS, 2, R // 4], I32, "stage")

        cq_t = [load_cq(0)]
        l1 = load_list(offs, "l1")
        gs_t = load_rows(gs, "gs_t")
        for s, src in enumerate((w_scales, w2_scales)):
            nc.sync.dma_start(stage[:, :, s, :], src[0].bitcast(I32).rearrange("(q r) n -> r q n", r=LIVE))
        cq_t.append(load_cq(1))
        cq_t.append(load_cq(2))
        l2 = load_list(offs2, "l2")
        cq_t.append(load_cq(3))
        load_plane(xo_s, xo_scales)
        w_raw = load_fp4(w_words, "w_raw")
        xo_w = load_fp8(xo_words, "xo_w")
        w2_raw = load_fp4(w2_words, "w2_raw")
        l3 = load_list(offs3, "l3")
        l4 = load_list(offs4, "l4")
        sa_t = load_rows(sa, "sa_t")
        l5 = load_list(offs5, "l5")
        sb_t = load_rows(sb, "sb_t")
        l6 = load_list(offs6, "l6")
        sg_t = load_rows(sg, "sg_t")
        bg_t = load_rows(bg, "bg_t")
        ws_w = load_fp4(ws_words, "ws_w")
        sx_w = load_fp8(sx_words, "sx_w")
        wb_w = load_fp4(wb_words, "wb_w")
        l7 = load_list(offs7, "l7")
        load_plane(ws_s, ws_scales)
        load_plane(sx_s, sx_scales)
        load_plane(wb_s, wb_scales)

        warm = new([P, 2], F32, "warm")
        nc.vector.memset(warm[:, 0:1], 0.0)
        nc.scalar.activation(out=warm[:, 1:2], in_=warm[:, 0:1], func=ACT.Sigmoid)

        raw_s = new([P, 2, R], U8, "raw_s")
        raw_words = raw_s[:].rearrange("p s c -> p (s c)").bitcast(I32)
        nc.vector.memset(raw_words, 0)
        for q in range(QUADS):
            nc.vector.tensor_copy(
                raw_words[QROWS * q:QROWS * q + LIVE, :], stage[:, q, :, :].rearrange("p s c -> p (s c)"),
            )

        def deal_scales(s, name):
            dealt = new([P, R], U8, name)
            nc.vector.tensor_copy(
                dealt[:].rearrange("p (t c i) -> p c t i", t=PACK, i=16),
                raw_s[:, s, :].rearrange("p (c i t) -> p c t i", t=PACK, i=16),
            )
            return dealt

        def deal_words(raw, name):
            dealt = new([P, 2 * R], U8, name)
            nc.scalar.copy(
                dealt[:].bitcast(U16).rearrange("p (t c i) -> p c t i", t=PACK, i=8),
                raw[:].bitcast(U16).rearrange("p (c i t) -> p c t i", t=PACK, i=8),
            )
            return dealt

        w_s = deal_scales(0, "w_s")
        w2_s = deal_scales(1, "w2_s")
        xg_s = new([P, J], U8, "xg_s")
        nc.vector.tensor_copy(xg_s[:], xo_s[:].indirect(l2[:]))

        x1 = new([P, PACK, J], BF16, "x1")
        x1_il = new([P, J, PACK], BF16, "x1_il")
        x1_c = new([P, J], U32, "x1_c")
        x1_s = new([P, J], U8, "x1_s")
        for t in range(PACK):
            nc.scalar.activation(
                out=x1[:, t, :], in_=cq_t[t][:].indirect(l1[:]), func=ACT.Copy, scale=gs_t[:, t:t + 1],
            )
        w_d = deal_words(w_raw, "w_d")
        halves = [slice(0, J // 2), slice(J // 2, J)]
        for h in halves:
            nc.vector.tensor_copy(
                x1_il[:, h, :].rearrange("p (c i) t -> p c t i", i=4),
                x1[:, :, h].rearrange("p t (c i) -> p c t i", i=4),
            )
        for h in halves:
            nc.vector.quantize_mx(
                out=x1_c[:, h].bitcast(FP8X4), scales=x1_s[:, h],
                in_=x1_il[:, h, :].rearrange("p j t -> p (j t)"),
            )
        w2_d = deal_words(w2_raw, "w2_d")

        a_ps = [psum.tile([P, J], F32, name="a_ps%d" % t, tag="a_ps%d" % t) for t in range(PACK)]
        for t in range(PACK):
            nc.tensor.matmul_mx(
                out=a_ps[t][:], lhsT=w_d[:, 2 * P * t:2 * P * (t + 1)].bitcast(FP4X4),
                lhsT_scale=w_s[:, P * t:P * (t + 1)], rhs=x1_c[:].bitcast(FP8X4), rhs_scale=x1_s[:],
                start=True, stop=True,
            )

        xg_w = new([P, J], U32, "xg_w")
        nc.vector.tensor_copy(xg_w[:], xo_w[:].indirect(l2[:]))
        b_ps = [psum.tile([P, J], F32, name="b_ps%d" % t) for t in range(PACK)]
        for t in range(PACK):
            nc.tensor.matmul_mx(
                out=b_ps[t][:], lhsT=w2_d[:, 2 * P * t:2 * P * (t + 1)].bitcast(FP4X4),
                lhsT_scale=w2_s[:, P * t:P * (t + 1)], rhs=xg_w[:].bitcast(FP8X4), rhs_scale=xg_s[:],
                start=True, stop=True,
            )

        pw = [new([P, C], F32, "pw%d" % t) for t in range(PACK)]
        picked = [new([P, J], F32, "picked%d" % t) for t in range(PACK)]
        rb = [new([P, J], F32, "rb%d" % t) for t in range(PACK)]
        val = new([P, PACK, O], F32, "val")
        gate = new([P, PACK, O], F32, "gate")
        for t in range(PACK):
            nc.vector.memset(pw[t][:], 0.0)

        def pick(t):
            nc.scalar.activation(out=picked[t][:], in_=pw[t][:].indirect(l4[:]), func=ACT.Copy, scale=sa_t[:, t:t + 1])

        def larger(t):
            nc.vector.tensor_tensor(out=rb[t][:], in0=b_ps[t][:], in1=picked[t][:], op=ALU.max)

        def look(t):
            nc.scalar.activation(out=val[:, t, :], in_=rb[t][:].indirect(l5[:]), func=ACT.Copy, scale=sb_t[:, t:t + 1])
            nc.scalar.activation(
                out=gate[:, t, :], in_=rb[t][:].indirect(l6[:]), func=ACT.Sigmoid,
                scale=sg_t[:, t:t + 1], bias=bg_t[:, t:t + 1],
            )

        half = J // 2
        a_sb = [new([P, J], F32, "a_sb%d" % t, "xo_w" if t == 0 else None) for t in range(PACK)]
        nc.vector.tensor_copy(a_sb[0][:], a_ps[0][:])
        nc.scalar.copy(a_sb[1][:], a_ps[1][:])
        nc.vector.tensor_copy(pw[0][:].indirect(l3[:]), a_sb[0][:])
        nc.scalar.activation(out=pw[1][:].indirect(l3[:]), in_=a_sb[1][:], func=ACT.Copy)
        nc.vector.tensor_copy(a_sb[2][:], a_ps[2][:])
        nc.vector.tensor_copy(a_sb[3][:], a_ps[3][:])
        nc.vector.tensor_copy(pw[2][:].indirect(l3[:]), a_sb[2][:])
        pick(0)
        pick(1)
        nc.scalar.activation(out=pw[3][:].indirect(l3[:, 0:half // 16]), in_=a_sb[3][:, 0:half], func=ACT.Copy)
        larger(0)
        nc.vector.tensor_copy(pw[3][:].indirect(l3[:, half // 16:J // 16]), a_sb[3][:, half:J])
        pick(2)
        look(0)
        larger(1)
        pick(3)
        larger(2)
        larger(3)
        for t in range(1, PACK):
            look(t)

        hid_il = new([P, O, PACK], BF16, "hid_il")
        nc.vector.tensor_tensor(
            out=hid_il[:].rearrange("p (c i) t -> p c t i", i=4),
            in0=val[:].rearrange("p t (c i) -> p c t i", i=4),
            in1=gate[:].rearrange("p t (c i) -> p c t i", i=4),
            op=ALU.mult,
        )
        hid_c = new([P, O], U32, "hid_c")
        hid_s = new([P, O], U8, "hid_s")
        nc.vector.quantize_mx(
            out=hid_c[:].bitcast(FP8X4), scales=hid_s[:], in_=hid_il[:].rearrange("p o t -> p (o t)"),
        )

        p_ps = [psum.tile([P, O], F32, name="p_ps%d" % h, tag="a_ps%d" % (2 + h)) for h in range(N // P)]
        for h in range(N // P):
            nc.tensor.matmul_mx(
                out=p_ps[h][:], lhsT=ws_w[:, 2 * P * h:2 * P * (h + 1)].bitcast(FP4X4),
                lhsT_scale=ws_s[:, P * h:P * (h + 1)], rhs=sx_w[:].bitcast(FP8X4), rhs_scale=sx_s[:],
                start=True, stop=False,
            )
        for h in range(N // P):
            nc.tensor.matmul_mx(
                out=p_ps[h][:], lhsT=wb_w[:, 2 * P * h:2 * P * (h + 1)].bitcast(FP4X4),
                lhsT_scale=wb_s[:, P * h:P * (h + 1)], rhs=hid_c[:].bitcast(FP8X4), rhs_scale=hid_s[:],
                start=False, stop=True,
            )

        page = [new([P, E], F32, "page%d" % h) for h in range(N // P)]
        p_sb = [new([P, O], F32, "p_sb%d" % h) for h in range(N // P)]
        for h in range(N // P):
            nc.vector.memset(page[h][:], 0.0)
        nc.vector.tensor_copy(p_sb[0][:], p_ps[0][:])
        nc.vector.tensor_copy(page[0][:].indirect(l7[:]), p_sb[0][:])
        nc.scalar.copy(p_sb[1][:], p_ps[1][:])
        nc.scalar.activation(out=page[1][:].indirect(l7[:]), in_=p_sb[1][:], func=ACT.Copy)
        for h in range(N // P):
            nc.sync.dma_start(out[P * h:P * (h + 1), :], page[h][:])
